import numpy as np
import ml_dtypes


def mxq(x, axis, fmt="e4m3"):
    dtype, down = {"e4m3": (ml_dtypes.float8_e4m3fn, 7), "e5m2": (ml_dtypes.float8_e5m2, 14)}[fmt]
    v = np.moveaxis(np.asarray(x, np.float32).astype(ml_dtypes.bfloat16).astype(np.float64), axis, -1)
    blocks = v.reshape(v.shape[:-1] + (-1, 32))
    amax = np.abs(blocks).max(-1, keepdims=True)
    byte = np.maximum(np.where(amax > 0, np.frexp(amax)[1] - 1 + 127, 0) - down, 1)
    scale = np.exp2(byte - 127.0)
    codes = (blocks / scale).astype(np.float32).astype(dtype).astype(np.float64)
    return np.moveaxis((codes * scale).reshape(v.shape), -1, axis)


WIDE = False


def mx_kscale(k):
    if not WIDE:
        return np.ones(k)
    levels = np.array([10, -10, 5, -5, 0])
    if k % 512:
        return np.exp2(np.random.permutation(np.resize(levels, k // 32))).repeat(32)
    a = np.empty((k // 512, 16))
    for p in range(k // 512):
        a[p, :8] = np.random.permutation(np.resize(levels, 8))
        for g in range(8):
            far = levels[np.abs(levels - a[p, g]) >= 10]
            a[p, g + 8] = far[np.random.randint(len(far))]
    return np.exp2(a.ravel()).repeat(32)


def f64(x):
    return np.asarray(x).astype(np.float64)


def striped(idx):
    return np.tile(idx.reshape(-1, 16).T, (8, 1)).astype(np.uint16)


def unstriped(offs):
    return offs[:16].T.reshape(-1).astype(np.int64)


def pack_weight(w):
    k, n = w.shape
    w = f64(np.asarray(w, np.float32).astype(ml_dtypes.bfloat16)).reshape(k // 32, 32, n)
    amax = np.abs(w).max(1)
    byte = np.clip(np.where(amax > 0, np.frexp(amax)[1] - 1 + 127 - 7, 1), 1, 254)
    scaled = (w * np.exp2(127.0 - byte)[:, None, :]).reshape(k, n).astype(np.float32)
    words = np.ascontiguousarray(scaled.reshape(k // 512, 128, 4, n).transpose(0, 1, 3, 2)).astype(ml_dtypes.float8_e4m3fn).view(np.uint8)
    return words, np.ascontiguousarray(byte.astype(np.uint8).reshape(k // 512, 16, n))


def unpack_weight(words, scales):
    g, p, n, _ = words.shape
    vals = np.ascontiguousarray(words).view(ml_dtypes.float8_e4m3fn).astype(np.float64) * np.repeat(np.exp2(scales.astype(np.float64) - 127.0), 8, axis=1)[..., None]
    return vals.transpose(0, 1, 3, 2).reshape(g * 512, n)


K, T, S, N = 1024, 2048, 1024, 256
P = 2 ** 7


def setup_inputs():
    n = np.random.standard_normal
    s = mx_kscale(K)[:, None]
    packed_xT = pack_weight(n((K, T)) * s)
    return {
        "x_words": packed_xT[0],
        "x_scales": packed_xT[1],
        "w1": (n((K, N)) / np.sqrt(K) / s).astype(np.float32),
        "truth": (np.random.uniform(0.3, 3.0, (N, S))).astype(np.float32),
        "valid": (np.tile(np.random.uniform(0.2, 1.0, S), (P, 1))).astype(np.float32),
        "offs": striped(np.random.permutation(T)[:S]),
    }


def reference(x_words, x_scales, w1, truth, valid, offs):
    xq = unpack_weight(x_words, x_scales)[:, unstriped(offs)]
    y = mxq(f64(w1), 0, "e4m3").T @ xq
    ld = y - (np.log(f64(truth)))
    ldm = ld.mean(axis=1, keepdims=True)
    ld2 = (ld) ** 2
    sil = ld2.mean(axis=1, keepdims=True) - (0.85 * ((ldm) ** 2)) + 0.05
    return f64(valid)[:1] * ((ld - (0.85 * ldm)) / np.sqrt(sil))

@@ -1,0 +1,171 @@
+from contextlib import ExitStack
+
+import concourse.mybir as mybir
+from concourse.masks import make_identity
+
+K, T, S, N = 1024, 2048, 1024, 256
+FLOPS = 2 * K * S * N
+
+F32 = mybir.dt.float32
+BF16 = mybir.dt.bfloat16
+I32 = mybir.dt.int32
+U32 = mybir.dt.uint32
+U16 = mybir.dt.uint16
+U8 = mybir.dt.uint8
+FP8X4 = mybir.dt.float8_e4m3fn_x4
+ACT = mybir.ActivationFunctionType
+ALU = mybir.AluOpType
+
+P = 128
+PACK = 4
+PASSES = K // (P * PACK)
+HALF = 512
+HALVES = S // HALF
+BLOCKS = N // P
+LIST_COLS = HALF // 16
+QUADRANTS = 4
+LAMBDA = 0.85
+EPS = 0.05
+
+
+def tile_picked_yslog_grad_p_kernel(tc, x_words, x_scales, w1, truth, valid, offs, out):
+    nc = tc.nc
+    with ExitStack() as ctx:
+        keep = ctx.enter_context(tc.tile_pool(name="keep", bufs=1))
+        psum = ctx.enter_context(tc.psum_pool(name="psum", bufs=1))
+
+        offsets = keep.tile([P, S // 16], U16, name="offsets")
+        nc.sync.dma_start(offsets[:], offs)
+
+        scale_window = keep.tile([P, T], U8, name="scale_window", align_bytes=64)
+        nc.vector.memset(scale_window[:].bitcast(I32), 0)
+
+        word_window = [keep.tile([P, T], U32, name="word_window%d" % o, align_bytes=64) for o in range(PASSES)]
+
+        def load_words(o):
+            nc.sync.dma_start(word_window[o][:].bitcast(I32), x_words[o].rearrange("p c r -> p (c r)").bitcast(I32))
+
+        load_words(0)
+        for q in range(QUADRANTS):
+            nc.sync.dma_start(
+                scale_window[32 * q : 32 * q + PACK * PASSES, :].bitcast(I32),
+                x_scales[:, PACK * q : PACK * (q + 1), :].bitcast(I32),
+            )
+        valid_cols = keep.tile([P, HALVES, 8], F32, name="valid_cols")
+        nc.sync.dma_start(valid_cols[:, :, 0:PACK], valid[0].rearrange("(h p c) -> p h c", h=HALVES, c=PACK))
+        w_raw = [keep.tile([P, PACK, N], F32, name="w_raw%d" % o, align_bytes=64) for o in range(PASSES)]
+        for o in range(PASSES):
+            nc.sync.dma_start(w_raw[o][:], w1[512 * o : 512 * (o + 1), :].rearrange("(p j) m -> p j m", j=PACK))
+        load_words(1)
+        truth_sb = {}
+        for b in range(BLOCKS):
+            for h in range(HALVES):
+                truth_sb[b, h] = keep.tile([P, HALF], F32, name="truth%d%d" % (b, h))
+                nc.sync.dma_start(truth_sb[b, h][:], truth[P * b : P * (b + 1), HALF * h : HALF * (h + 1)])
+
+        identity = keep.tile([P, P], F32, name="identity")
+        make_identity(nc, identity[:])
+        minus_half = keep.tile([P, 1], F32, name="minus_half")
+        nc.gpsimd.memset(minus_half[:], -0.5)
+
+        valid_bank = []
+        for h in range(HALVES):
+            bank = psum.tile([P, PACK, P], F32, name="valid_bank%d" % h)
+            for c in range(PACK):
+                nc.tensor.transpose(bank[:, c, :], valid_cols[:, h, c : c + 1].to_broadcast([P, P]), identity[:])
+            valid_bank.append(bank)
+
+        x_codes = {}
+
+        def gather_words(o, h):
+            x_codes[o, h] = keep.tile([P, HALF], U32, name="x_codes%d%d" % (o, h), align_bytes=64)
+            nc.vector.tensor_copy(
+                x_codes[o, h][:], word_window[o][:].indirect(offsets[:, LIST_COLS * h : LIST_COLS * (h + 1)])
+            )
+
+        for h in range(HALVES):
+            gather_words(0, h)
+        x_planes = keep.tile([P, S], U8, name="x_planes", align_bytes=64)
+        nc.vector.tensor_copy(x_planes[:], scale_window[:].indirect(offsets[:]))
+
+        w_codes, w_scales = [], []
+        for o in range(PASSES):
+            grouped = keep.tile([P, N, PACK], BF16, name="grouped%d" % o, align_bytes=64)
+            nc.scalar.copy(
+                grouped[:].rearrange("p (c i) j -> p c j i", i=4),
+                w_raw[o][:].rearrange("p j (c i) -> p c j i", i=4),
+            )
+            codes = keep.tile([P, N], U32, name="w_codes%d" % o, align_bytes=64)
+            scales = keep.tile([P, N], U8, name="w_scales%d" % o, align_bytes=64)
+            nc.vector.quantize_mx(out=codes[:].bitcast(FP8X4), scales=scales[:], in_=grouped[:].rearrange("p m j -> p (m j)"))
+            w_codes.append(codes)
+            w_scales.append(scales)
+
+        y_bank = {(b, h): psum.tile([P, HALF], F32, name="y%d%d" % (b, h)) for b in range(BLOCKS) for h in range(HALVES)}
+
+        def multiply(o, b, h):
+            nc.tensor.matmul_mx(
+                out=y_bank[b, h][:],
+                lhsT=w_codes[o][:, P * b : P * (b + 1)].bitcast(FP8X4),
+                lhsT_scale=w_scales[o][:, P * b : P * (b + 1)],
+                rhs=x_codes[o, h][:].bitcast(FP8X4),
+                rhs_scale=x_planes[PACK * o :, HALF * h : HALF * (h + 1)],
+                start=(o == 0),
+                stop=(o == PASSES - 1),
+            )
+
+        for h in range(HALVES):
+            for b in range(BLOCKS):
+                multiply(0, b, h)
+
+        for h in range(HALVES):
+            gather_words(1, h)
+            for b in range(BLOCKS):
+                multiply(1, b, h)
+
+        log_truth = {}
+        for b in range(BLOCKS):
+            for h in range(HALVES):
+                log_truth[b, h] = keep.tile([P, HALF], F32, name="log_truth%d%d" % (b, h))
+                nc.scalar.activation(log_truth[b, h][:], truth_sb[b, h][:], ACT.Ln)
+
+        ld, shift, rstd = {}, {}, {}
+        for b in range(BLOCKS):
+            sums = keep.tile([P, HALVES], F32, name="sums%d" % b)
+            squares = keep.tile([P, HALVES], F32, name="squares%d" % b)
+            for h in range(HALVES):
+                ld[b, h] = keep.tile([P, HALF], F32, name="ld%d%d" % (b, h))
+                nc.vector.scalar_tensor_tensor(
+                    ld[b, h][:], y_bank[b, h][:], 1.0, log_truth[b, h][:], ALU.mult, ALU.subtract,
+                    accum_out=sums[:, h : h + 1],
+                )
+                squared = keep.tile([P, HALF], F32, name="squared%d%d" % (b, h))
+                nc.scalar.activation(
+                    squared[:], ld[b, h][:], ACT.Square, scale=1.0 / 32, accum_out=squares[:, h : h + 1]
+                )
+            stats = keep.tile([P, 5], F32, name="stats%d" % b)
+            shift[b] = stats[:, 0:1]
+            rstd[b] = stats[:, 4:5]
+            nc.gpsimd.tensor_scalar(shift[b], sums[:, 0:1], sums[:, 1:2], -LAMBDA / S, ALU.add, ALU.mult)
+            nc.gpsimd.tensor_scalar(stats[:, 1:2], shift[b], shift[b], -1.0 / LAMBDA, ALU.mult, ALU.mult)
+            nc.gpsimd.tensor_scalar(stats[:, 2:3], squares[:, 0:1], stats[:, 1:2], EPS, ALU.add, ALU.add)
+            nc.gpsimd.tensor_tensor(stats[:, 3:4], squares[:, 1:2], stats[:, 2:3], ALU.add)
+            nc.gpsimd.tensor_tensor(rstd[b], stats[:, 3:4], minus_half[:], ALU.pow)
+
+        for b in range(BLOCKS):
+            for h in range(HALVES):
+                weighted = keep.tile([P, HALF], F32, name="weighted%d%d" % (b, h))
+                nc.vector.scalar_tensor_tensor(
+                    weighted[:].rearrange("q (p c) -> q p c", c=PACK),
+                    ld[b, h][:].rearrange("q (p c) -> q p c", c=PACK),
+                    shift[b],
+                    valid_bank[h][:].rearrange("q c p -> q p c"),
+                    ALU.add,
+                    ALU.mult,
+                )
+                result = keep.tile([P, HALF], F32, name="result%d%d" % (b, h))
+                if (b, h) == (BLOCKS - 1, HALVES - 1):
+                    nc.vector.tensor_scalar(result[:], weighted[:], rstd[b], None, ALU.mult)
+                else:
+                    nc.scalar.activation(result[:], weighted[:], ACT.Copy, scale=rstd[b])
+                nc.sync.dma_start(out[P * b : P * (b + 1), HALF * h : HALF * (h + 1)], result[:])

@@ -1,3 +1,4 @@
+import math
 from contextlib import ExitStack
 
 import concourse.mybir as mybir
@@ -63,16 +64,20 @@ def tile_picked_yslog_grad_p_kernel(tc, x_words, x_scales, w1, truth, valid, off
                 truth_sb[b, h] = keep.tile([P, HALF], F32, name="truth%d%d" % (b, h))
                 nc.sync.dma_start(truth_sb[b, h][:], truth[P * b : P * (b + 1), HALF * h : HALF * (h + 1)])
 
-        identity = keep.tile([P, P], F32, name="identity")
-        make_identity(nc, identity[:])
         minus_half = keep.tile([P, 1], F32, name="minus_half")
         nc.gpsimd.memset(minus_half[:], -0.5)
+        table_warm = keep.tile([P, 1], F32, name="table_warm")
+        nc.scalar.activation(table_warm[:], minus_half[:], ACT.Ln, scale=-1.0)
+        identity = keep.tile([P, P], F32, name="identity")
+        make_identity(nc, identity[:])
 
+        valid_scaled = keep.tile([P, HALVES, PACK], F32, name="valid_scaled")
+        nc.scalar.activation(valid_scaled[:], valid_cols[:, :, 0:PACK], ACT.Copy, scale=S / math.sqrt(LAMBDA))
         valid_bank = []
         for h in range(HALVES):
             bank = psum.tile([P, PACK, P], F32, name="valid_bank%d" % h)
             for c in range(PACK):
-                nc.tensor.transpose(bank[:, c, :], valid_cols[:, h, c : c + 1].to_broadcast([P, P]), identity[:])
+                nc.tensor.transpose(bank[:, c, :], valid_scaled[:, h, c : c + 1].to_broadcast([P, P]), identity[:])
             valid_bank.append(bank)
 
         x_codes = {}
@@ -85,12 +90,18 @@ def tile_picked_yslog_grad_p_kernel(tc, x_words, x_scales, w1, truth, valid, off
 
         for h in range(HALVES):
             gather_words(0, h)
-        x_planes = keep.tile([P, S], U8, name="x_planes", align_bytes=64)
-        nc.vector.tensor_copy(x_planes[:], scale_window[:].indirect(offsets[:]))
+        x_planes = {}
 
+        def gather_scales(h, tag):
+            x_planes[h] = keep.tile([P, HALF], U8, name="x_planes%d" % h, tag=tag, align_bytes=64)
+            nc.vector.tensor_copy(
+                x_planes[h][:], scale_window[:].indirect(offsets[:, LIST_COLS * h : LIST_COLS * (h + 1)])
+            )
+
+        gather_scales(0, "x_planes0")
         w_codes, w_scales = [], []
         for o in range(PASSES):
-            grouped = keep.tile([P, N, PACK], BF16, name="grouped%d" % o, align_bytes=64)
+            grouped = keep.tile([P, N, PACK], BF16, name="grouped%d" % o, tag="grouped%d" % o, align_bytes=64)
             nc.scalar.copy(
                 grouped[:].rearrange("p (c i) j -> p c j i", i=4),
                 w_raw[o][:].rearrange("p j (c i) -> p c j i", i=4),
@@ -100,6 +111,8 @@ def tile_picked_yslog_grad_p_kernel(tc, x_words, x_scales, w1, truth, valid, off
             nc.vector.quantize_mx(out=codes[:].bitcast(FP8X4), scales=scales[:], in_=grouped[:].rearrange("p m j -> p (m j)"))
             w_codes.append(codes)
             w_scales.append(scales)
+            if o == 0:
+                gather_scales(1, "grouped0")
 
         y_bank = {(b, h): psum.tile([P, HALF], F32, name="y%d%d" % (b, h)) for b in range(BLOCKS) for h in range(HALVES)}
 
@@ -109,7 +122,7 @@ def tile_picked_yslog_grad_p_kernel(tc, x_words, x_scales, w1, truth, valid, off
                 lhsT=w_codes[o][:, P * b : P * (b + 1)].bitcast(FP8X4),
                 lhsT_scale=w_scales[o][:, P * b : P * (b + 1)],
                 rhs=x_codes[o, h][:].bitcast(FP8X4),
-                rhs_scale=x_planes[PACK * o :, HALF * h : HALF * (h + 1)],
+                rhs_scale=x_planes[h][PACK * o :, :],
                 start=(o == 0),
                 stop=(o == PASSES - 1),
             )
@@ -129,43 +142,70 @@ def tile_picked_yslog_grad_p_kernel(tc, x_words, x_scales, w1, truth, valid, off
                 log_truth[b, h] = keep.tile([P, HALF], F32, name="log_truth%d%d" % (b, h))
                 nc.scalar.activation(log_truth[b, h][:], truth_sb[b, h][:], ACT.Ln)
 
+        chunks = [(b, h) for b in range(BLOCKS) for h in range(HALVES)]
         ld, shift, rstd = {}, {}, {}
-        for b in range(BLOCKS):
-            sums = keep.tile([P, HALVES], F32, name="sums%d" % b)
-            squares = keep.tile([P, HALVES], F32, name="squares%d" % b)
-            for h in range(HALVES):
-                ld[b, h] = keep.tile([P, HALF], F32, name="ld%d%d" % (b, h))
-                nc.vector.scalar_tensor_tensor(
-                    ld[b, h][:], y_bank[b, h][:], 1.0, log_truth[b, h][:], ALU.mult, ALU.subtract,
-                    accum_out=sums[:, h : h + 1],
-                )
-                squared = keep.tile([P, HALF], F32, name="squared%d%d" % (b, h))
-                nc.scalar.activation(
-                    squared[:], ld[b, h][:], ACT.Square, scale=1.0 / 32, accum_out=squares[:, h : h + 1]
-                )
-            stats = keep.tile([P, 5], F32, name="stats%d" % b)
-            shift[b] = stats[:, 0:1]
-            rstd[b] = stats[:, 4:5]
-            nc.gpsimd.tensor_scalar(shift[b], sums[:, 0:1], sums[:, 1:2], -LAMBDA / S, ALU.add, ALU.mult)
-            nc.gpsimd.tensor_scalar(stats[:, 1:2], shift[b], shift[b], -1.0 / LAMBDA, ALU.mult, ALU.mult)
-            nc.gpsimd.tensor_scalar(stats[:, 2:3], squares[:, 0:1], stats[:, 1:2], EPS, ALU.add, ALU.add)
-            nc.gpsimd.tensor_tensor(stats[:, 3:4], squares[:, 1:2], stats[:, 2:3], ALU.add)
-            nc.gpsimd.tensor_tensor(rstd[b], stats[:, 3:4], minus_half[:], ALU.pow)
+        sums = [keep.tile([P, HALVES], F32, name="sums%d" % b) for b in range(BLOCKS)]
+        squares = [keep.tile([P, HALVES], F32, name="squares%d" % b) for b in range(BLOCKS)]
+        result = {c: keep.tile([P, HALF], F32, name="result%d%d" % c) for c in chunks}
 
-        for b in range(BLOCKS):
-            for h in range(HALVES):
-                weighted = keep.tile([P, HALF], F32, name="weighted%d%d" % (b, h))
-                nc.vector.scalar_tensor_tensor(
-                    weighted[:].rearrange("q (p c) -> q p c", c=PACK),
-                    ld[b, h][:].rearrange("q (p c) -> q p c", c=PACK),
-                    shift[b],
-                    valid_bank[h][:].rearrange("q c p -> q p c"),
-                    ALU.add,
-                    ALU.mult,
-                )
-                result = keep.tile([P, HALF], F32, name="result%d%d" % (b, h))
-                if (b, h) == (BLOCKS - 1, HALVES - 1):
-                    nc.vector.tensor_scalar(result[:], weighted[:], rstd[b], None, ALU.mult)
-                else:
-                    nc.scalar.activation(result[:], weighted[:], ACT.Copy, scale=rstd[b])
-                nc.sync.dma_start(out[P * b : P * (b + 1), HALF * h : HALF * (h + 1)], result[:])
+        def mirrored(b, h):
+            return (BLOCKS - 1 - b, HALVES - 1 - h)
+
+        def difference(b, h):
+            ld[b, h] = keep.tile([P, HALF], F32, name="ld%d%d" % (b, h))
+            nc.vector.scalar_tensor_tensor(
+                ld[b, h][:], y_bank[b, h][:], 1.0, log_truth[b, h][:], ALU.mult, ALU.subtract,
+                accum_out=sums[b][:, h : h + 1],
+            )
+
+        def square(b, h):
+            nc.scalar.activation(
+                result[mirrored(b, h)][:], ld[b, h][:], ACT.Square, scale=math.sqrt(S / LAMBDA),
+                accum_out=squares[b][:, h : h + 1],
+            )
+
+        def statistics(b):
+            total_squared = keep.tile([P, 1], F32, name="total_squared%d" % b)
+            nc.scalar.activation(total_squared[:], sums[b][:, 1:2], ACT.Square, bias=sums[b][:, 0:1])
+            square(b, 1)
+            stats = keep.tile([P, 3], F32, name="stats%d" % b)
+            nc.gpsimd.tensor_scalar(
+                stats[:, 0:1], squares[b][:, 0:1], total_squared[:], EPS * S * S / LAMBDA, ALU.subtract, ALU.add
+            )
+            nc.gpsimd.tensor_tensor(stats[:, 1:2], stats[:, 0:1], squares[b][:, 1:2], ALU.add)
+            rstd[b] = stats[:, 2:3]
+            nc.gpsimd.tensor_tensor(rstd[b], stats[:, 1:2], minus_half[:], ALU.pow)
+
+        def mean_shift(b):
+            shift[b] = keep.tile([P, 1], F32, name="shift%d" % b)
+            nc.vector.tensor_scalar(shift[b][:], sums[b][:, 0:1], sums[b][:, 1:2], -LAMBDA / S, ALU.add, ALU.mult)
+
+        def finish(b, h):
+            weighted = log_truth[mirrored(b, h)]
+            nc.vector.scalar_tensor_tensor(
+                weighted[:].rearrange("q (p c) -> q p c", c=PACK),
+                ld[b, h][:].rearrange("q (p c) -> q p c", c=PACK),
+                shift[b][:],
+                valid_bank[h][:].rearrange("q c p -> q p c"),
+                ALU.add,
+                ALU.mult,
+            )
+            if (b, h) == chunks[-1]:
+                nc.vector.tensor_scalar(result[b, h][:], weighted[:], rstd[b], None, ALU.mult)
+            else:
+                nc.scalar.activation(result[b, h][:], weighted[:], ACT.Copy, scale=rstd[b])
+            nc.sync.dma_start(out[P * b : P * (b + 1), HALF * h : HALF * (h + 1)], result[b, h][:])
+
+        difference(0, 0)
+        square(0, 0)
+        difference(0, 1)
+        statistics(0)
+        difference(1, 0)
+        square(1, 0)
+        mean_shift(0)
+        difference(1, 1)
+        statistics(1)
+        finish(0, 0)
+        mean_shift(1)
+        for b, h in chunks[1:]:
+            finish(b, h)

@@ -36,7 +36,6 @@ def tile_picked_yslog_grad_p_kernel(tc, x_words, x_scales, w1, truth, valid, off
         psum = ctx.enter_context(tc.psum_pool(name="psum", bufs=1))
 
         offsets = keep.tile([P, S // 16], U16, name="offsets")
-        nc.sync.dma_start(offsets[:], offs)
 
         scale_window = keep.tile([P, T], U8, name="scale_window", align_bytes=64)
         nc.vector.memset(scale_window[:].bitcast(I32), 0)
@@ -47,13 +46,15 @@ def tile_picked_yslog_grad_p_kernel(tc, x_words, x_scales, w1, truth, valid, off
             nc.sync.dma_start(word_window[o][:].bitcast(I32), x_words[o].rearrange("p c r -> p (c r)").bitcast(I32))
 
         load_words(0)
+        nc.sync.dma_start(offsets[:], offs)
         for q in range(QUADRANTS):
             nc.sync.dma_start(
                 scale_window[32 * q : 32 * q + PACK * PASSES, :].bitcast(I32),
                 x_scales[:, PACK * q : PACK * (q + 1), :].bitcast(I32),
             )
-        valid_cols = keep.tile([P, HALVES, 8], F32, name="valid_cols")
-        nc.sync.dma_start(valid_cols[:, :, 0:PACK], valid[0].rearrange("(h p c) -> p h c", h=HALVES, c=PACK))
+        valid_rows = keep.tile([P, P], F32, name="valid_rows")
+        nc.gpsimd.memset(valid_rows[:], 0.0)
+        nc.sync.dma_start(valid_rows[0 : S // P, :], valid[0].rearrange("(c p) -> c p", p=P))
         w_raw = [keep.tile([P, PACK, N], F32, name="w_raw%d" % o, align_bytes=64) for o in range(PASSES)]
         for o in range(PASSES):
             nc.sync.dma_start(w_raw[o][:], w1[512 * o : 512 * (o + 1), :].rearrange("(p j) m -> p j m", j=PACK))
@@ -71,13 +72,18 @@ def tile_picked_yslog_grad_p_kernel(tc, x_words, x_scales, w1, truth, valid, off
         identity = keep.tile([P, P], F32, name="identity")
         make_identity(nc, identity[:])
 
-        valid_scaled = keep.tile([P, HALVES, PACK], F32, name="valid_scaled")
-        nc.scalar.activation(valid_scaled[:], valid_cols[:, :, 0:PACK], ACT.Copy, scale=S / math.sqrt(LAMBDA))
+        turned = psum.tile([P, P], F32, name="turned")
+        nc.tensor.transpose(turned[:], valid_rows[:], identity[:])
+        valid_scaled = keep.tile([P, S // P], F32, name="valid_scaled")
+        nc.scalar.activation(valid_scaled[:], turned[:, 0 : S // P], ACT.Copy, scale=S / math.sqrt(LAMBDA))
         valid_bank = []
         for h in range(HALVES):
-            bank = psum.tile([P, PACK, P], F32, name="valid_bank%d" % h)
-            for c in range(PACK):
-                nc.tensor.transpose(bank[:, c, :], valid_scaled[:, h, c : c + 1].to_broadcast([P, P]), identity[:])
+            bank = psum.tile([P, HALF], F32, name="valid_bank%d" % h)
+            for c in range(HALF // P):
+                column = HALF // P * h + c
+                nc.tensor.transpose(
+                    bank[:, P * c : P * (c + 1)], valid_scaled[:, column : column + 1].to_broadcast([P, P]), identity[:]
+                )
             valid_bank.append(bank)
 
         x_codes = {}
@@ -183,10 +189,10 @@ def tile_picked_yslog_grad_p_kernel(tc, x_words, x_scales, w1, truth, valid, off
         def finish(b, h):
             weighted = log_truth[mirrored(b, h)]
             nc.vector.scalar_tensor_tensor(
-                weighted[:].rearrange("q (p c) -> q p c", c=PACK),
-                ld[b, h][:].rearrange("q (p c) -> q p c", c=PACK),
+                weighted[:],
+                ld[b, h][:],
                 shift[b][:],
-                valid_bank[h][:].rearrange("q c p -> q p c"),
+                valid_bank[h][:],
                 ALU.add,
                 ALU.mult,
             )

@@ -45,20 +45,19 @@ def tile_picked_yslog_grad_p_kernel(tc, x_words, x_scales, w1, truth, valid, off
         def load_words(o):
             nc.sync.dma_start(word_window[o][:].bitcast(I32), x_words[o].rearrange("p c r -> p (c r)").bitcast(I32))
 
-        load_words(0)
         nc.sync.dma_start(offsets[:], offs)
+        valid_rows = keep.tile([P, P], F32, name="valid_rows")
+        nc.gpsimd.memset(valid_rows[:], 0.0)
+        nc.sync.dma_start(valid_rows[0 : S // P, :], valid[0].rearrange("(c p) -> c p", p=P))
         for q in range(QUADRANTS):
             nc.sync.dma_start(
                 scale_window[32 * q : 32 * q + PACK * PASSES, :].bitcast(I32),
                 x_scales[:, PACK * q : PACK * (q + 1), :].bitcast(I32),
             )
-        valid_rows = keep.tile([P, P], F32, name="valid_rows")
-        nc.gpsimd.memset(valid_rows[:], 0.0)
-        nc.sync.dma_start(valid_rows[0 : S // P, :], valid[0].rearrange("(c p) -> c p", p=P))
         w_raw = [keep.tile([P, PACK, N], F32, name="w_raw%d" % o, align_bytes=64) for o in range(PASSES)]
         for o in range(PASSES):
+            load_words(o)
             nc.sync.dma_start(w_raw[o][:], w1[512 * o : 512 * (o + 1), :].rearrange("(p j) m -> p j m", j=PACK))
-        load_words(1)
         truth_sb = {}
         for b in range(BLOCKS):
             for h in range(HALVES):
@@ -94,41 +93,38 @@ def tile_picked_yslog_grad_p_kernel(tc, x_words, x_scales, w1, truth, valid, off
                 x_codes[o, h][:], word_window[o][:].indirect(offsets[:, LIST_COLS * h : LIST_COLS * (h + 1)])
             )
 
+        x_planes = keep.tile([P, S], U8, name="x_planes", align_bytes=64)
+        nc.vector.tensor_copy(x_planes[:], scale_window[:].indirect(offsets[:]))
         for h in range(HALVES):
             gather_words(0, h)
-        x_planes = {}
+        w_codes, w_scales = {}, {}
 
-        def gather_scales(h, tag):
-            x_planes[h] = keep.tile([P, HALF], U8, name="x_planes%d" % h, tag=tag, align_bytes=64)
-            nc.vector.tensor_copy(
-                x_planes[h][:], scale_window[:].indirect(offsets[:, LIST_COLS * h : LIST_COLS * (h + 1)])
-            )
-
-        gather_scales(0, "x_planes0")
-        w_codes, w_scales = [], []
-        for o in range(PASSES):
-            grouped = keep.tile([P, N, PACK], BF16, name="grouped%d" % o, tag="grouped%d" % o, align_bytes=64)
+        def quantize_weights(o, blocks):
+            width = P * len(blocks)
+            name = "%d%d" % (o, blocks[0])
+            grouped = keep.tile([P, width, PACK], BF16, name="grouped" + name, align_bytes=64)
             nc.scalar.copy(
                 grouped[:].rearrange("p (c i) j -> p c j i", i=4),
-                w_raw[o][:].rearrange("p j (c i) -> p c j i", i=4),
+                w_raw[o][:, :, P * blocks[0] : P * blocks[0] + width].rearrange("p j (c i) -> p c j i", i=4),
             )
-            codes = keep.tile([P, N], U32, name="w_codes%d" % o, align_bytes=64)
-            scales = keep.tile([P, N], U8, name="w_scales%d" % o, align_bytes=64)
+            codes = keep.tile([P, width], U32, name="w_codes" + name, align_bytes=64)
+            scales = keep.tile([P, width], U8, name="w_scales" + name, align_bytes=64)
             nc.vector.quantize_mx(out=codes[:].bitcast(FP8X4), scales=scales[:], in_=grouped[:].rearrange("p m j -> p (m j)"))
-            w_codes.append(codes)
-            w_scales.append(scales)
-            if o == 0:
-                gather_scales(1, "grouped0")
+            for n, b in enumerate(blocks):
+                w_codes[o, b] = codes[:, P * n : P * (n + 1)]
+                w_scales[o, b] = scales[:, P * n : P * (n + 1)]
+
+        quantize_weights(0, [0, 1])
 
         y_bank = {(b, h): psum.tile([P, HALF], F32, name="y%d%d" % (b, h)) for b in range(BLOCKS) for h in range(HALVES)}
 
         def multiply(o, b, h):
             nc.tensor.matmul_mx(
                 out=y_bank[b, h][:],
-                lhsT=w_codes[o][:, P * b : P * (b + 1)].bitcast(FP8X4),
-                lhsT_scale=w_scales[o][:, P * b : P * (b + 1)],
+                lhsT=w_codes[o, b].bitcast(FP8X4),
+                lhsT_scale=w_scales[o, b],
                 rhs=x_codes[o, h][:].bitcast(FP8X4),
-                rhs_scale=x_planes[h][PACK * o :, :],
+                rhs_scale=x_planes[PACK * o :, HALF * h : HALF * (h + 1)],
                 start=(o == 0),
                 stop=(o == PASSES - 1),
             )
@@ -139,7 +135,9 @@ def tile_picked_yslog_grad_p_kernel(tc, x_words, x_scales, w1, truth, valid, off
 
         for h in range(HALVES):
             gather_words(1, h)
-            for b in range(BLOCKS):
+        for b in range(BLOCKS):
+            quantize_weights(1, [b])
+            for h in range(HALVES):
                 multiply(1, b, h)
 
         log_truth = {}
@@ -196,7 +194,7 @@ def tile_picked_yslog_grad_p_kernel(tc, x_words, x_scales, w1, truth, valid, off
                 ALU.add,
                 ALU.mult,
             )
-            if (b, h) == chunks[-1]:
+            if b == BLOCKS - 1:
                 nc.vector.tensor_scalar(result[b, h][:], weighted[:], rstd[b], None, ALU.mult)
             else:
                 nc.scalar.activation(result[b, h][:], weighted[:], ACT.Copy, scale=rstd[b])

import math
from contextlib import ExitStack

import concourse.mybir as mybir
from concourse.masks import make_identity

K, T, S, N = 1024, 2048, 1024, 256
FLOPS = 2 * K * S * N

F32 = mybir.dt.float32
BF16 = mybir.dt.bfloat16
I32 = mybir.dt.int32
U32 = mybir.dt.uint32
U16 = mybir.dt.uint16
U8 = mybir.dt.uint8
FP8X4 = mybir.dt.float8_e4m3fn_x4
ACT = mybir.ActivationFunctionType
ALU = mybir.AluOpType

P = 128
PACK = 4
PASSES = K // (P * PACK)
HALF = 512
HALVES = S // HALF
BLOCKS = N // P
LIST_COLS = HALF // 16
QUADRANTS = 4
LAMBDA = 0.85
EPS = 0.05


def tile_picked_yslog_grad_p_kernel(tc, x_words, x_scales, w1, truth, valid, offs, out):
    nc = tc.nc
    with ExitStack() as ctx:
        keep = ctx.enter_context(tc.tile_pool(name="keep", bufs=1))
        psum = ctx.enter_context(tc.psum_pool(name="psum", bufs=1))

        offsets = keep.tile([P, S // 16], U16, name="offsets")

        scale_window = keep.tile([P, T], U8, name="scale_window", align_bytes=64)
        nc.vector.memset(scale_window[:].bitcast(I32), 0)

        word_window = [keep.tile([P, T], U32, name="word_window%d" % o, align_bytes=64) for o in range(PASSES)]

        def load_words(o):
            nc.sync.dma_start(word_window[o][:].bitcast(I32), x_words[o].rearrange("p c r -> p (c r)").bitcast(I32))

        nc.sync.dma_start(offsets[:], offs)
        valid_rows = keep.tile([P, P], F32, name="valid_rows")
        nc.gpsimd.memset(valid_rows[:], 0.0)
        nc.sync.dma_start(valid_rows[0 : S // P, :], valid[0].rearrange("(c p) -> c p", p=P))
        for q in range(QUADRANTS):
            nc.sync.dma_start(
                scale_window[32 * q : 32 * q + PACK * PASSES, :].bitcast(I32),
                x_scales[:, PACK * q : PACK * (q + 1), :].bitcast(I32),
            )
        w_raw = [keep.tile([P, PACK, N], F32, name="w_raw%d" % o, align_bytes=64) for o in range(PASSES)]
        for o in range(PASSES):
            load_words(o)
            nc.sync.dma_start(w_raw[o][:], w1[512 * o : 512 * (o + 1), :].rearrange("(p j) m -> p j m", j=PACK))
        truth_sb = {}
        for b in range(BLOCKS):
            for h in range(HALVES):
                truth_sb[b, h] = keep.tile([P, HALF], F32, name="truth%d%d" % (b, h))
                nc.sync.dma_start(truth_sb[b, h][:], truth[P * b : P * (b + 1), HALF * h : HALF * (h + 1)])

        minus_half = keep.tile([P, 1], F32, name="minus_half")
        nc.gpsimd.memset(minus_half[:], -0.5)
        table_warm = keep.tile([P, 1], F32, name="table_warm")
        nc.scalar.activation(table_warm[:], minus_half[:], ACT.Ln, scale=-1.0)
        identity = keep.tile([P, P], F32, name="identity")
        make_identity(nc, identity[:])

        turned = psum.tile([P, P], F32, name="turned")
        nc.tensor.transpose(turned[:], valid_rows[:], identity[:])
        valid_scaled = keep.tile([P, S // P], F32, name="valid_scaled")
        nc.scalar.activation(valid_scaled[:], turned[:, 0 : S // P], ACT.Copy, scale=S / math.sqrt(LAMBDA))
        valid_bank = []
        for h in range(HALVES):
            bank = psum.tile([P, HALF], F32, name="valid_bank%d" % h)
            for c in range(HALF // P):
                column = HALF // P * h + c
                nc.tensor.transpose(
                    bank[:, P * c : P * (c + 1)], valid_scaled[:, column : column + 1].to_broadcast([P, P]), identity[:]
                )
            valid_bank.append(bank)

        x_codes = {}

        def gather_words(o, h):
            x_codes[o, h] = keep.tile([P, HALF], U32, name="x_codes%d%d" % (o, h), align_bytes=64)
            nc.vector.tensor_copy(
                x_codes[o, h][:], word_window[o][:].indirect(offsets[:, LIST_COLS * h : LIST_COLS * (h + 1)])
            )

        x_planes = keep.tile([P, S], U8, name="x_planes", align_bytes=64)
        nc.vector.tensor_copy(x_planes[:], scale_window[:].indirect(offsets[:]))
        for h in range(HALVES):
            gather_words(0, h)
        w_codes, w_scales = {}, {}

        def quantize_weights(o, blocks):
            width = P * len(blocks)
            name = "%d%d" % (o, blocks[0])
            grouped = keep.tile([P, width, PACK], BF16, name="grouped" + name, align_bytes=64)
            nc.scalar.copy(
                grouped[:].rearrange("p (c i) j -> p c j i", i=4),
                w_raw[o][:, :, P * blocks[0] : P * blocks[0] + width].rearrange("p j (c i) -> p c j i", i=4),
            )
            codes = keep.tile([P, width], U32, name="w_codes" + name, align_bytes=64)
            scales = keep.tile([P, width], U8, name="w_scales" + name, align_bytes=64)
            nc.vector.quantize_mx(out=codes[:].bitcast(FP8X4), scales=scales[:], in_=grouped[:].rearrange("p m j -> p (m j)"))
            for n, b in enumerate(blocks):
                w_codes[o, b] = codes[:, P * n : P * (n + 1)]
                w_scales[o, b] = scales[:, P * n : P * (n + 1)]

        quantize_weights(0, [0, 1])

        y_bank = {(b, h): psum.tile([P, HALF], F32, name="y%d%d" % (b, h)) for b in range(BLOCKS) for h in range(HALVES)}

        def multiply(o, b, h):
            nc.tensor.matmul_mx(
                out=y_bank[b, h][:],
                lhsT=w_codes[o, b].bitcast(FP8X4),
                lhsT_scale=w_scales[o, b],
                rhs=x_codes[o, h][:].bitcast(FP8X4),
                rhs_scale=x_planes[PACK * o :, HALF * h : HALF * (h + 1)],
                start=(o == 0),
                stop=(o == PASSES - 1),
            )

        for h in range(HALVES):
            for b in range(BLOCKS):
                multiply(0, b, h)

        for h in range(HALVES):
            gather_words(1, h)
        for b in range(BLOCKS):
            quantize_weights(1, [b])
            for h in range(HALVES):
                multiply(1, b, h)

        log_truth = {}
        for b in range(BLOCKS):
            for h in range(HALVES):
                log_truth[b, h] = keep.tile([P, HALF], F32, name="log_truth%d%d" % (b, h))
                nc.scalar.activation(log_truth[b, h][:], truth_sb[b, h][:], ACT.Ln)

        chunks = [(b, h) for b in range(BLOCKS) for h in range(HALVES)]
        ld, shift, rstd = {}, {}, {}
        sums = [keep.tile([P, HALVES], F32, name="sums%d" % b) for b in range(BLOCKS)]
        squares = [keep.tile([P, HALVES], F32, name="squares%d" % b) for b in range(BLOCKS)]
        result = {c: keep.tile([P, HALF], F32, name="result%d%d" % c) for c in chunks}

        def mirrored(b, h):
            return (BLOCKS - 1 - b, HALVES - 1 - h)

        def difference(b, h):
            ld[b, h] = keep.tile([P, HALF], F32, name="ld%d%d" % (b, h))
            nc.vector.scalar_tensor_tensor(
                ld[b, h][:], y_bank[b, h][:], 1.0, log_truth[b, h][:], ALU.mult, ALU.subtract,
                accum_out=sums[b][:, h : h + 1],
            )

        def square(b, h):
            nc.scalar.activation(
                result[mirrored(b, h)][:], ld[b, h][:], ACT.Square, scale=math.sqrt(S / LAMBDA),
                accum_out=squares[b][:, h : h + 1],
            )

        def statistics(b):
            total_squared = keep.tile([P, 1], F32, name="total_squared%d" % b)
            nc.scalar.activation(total_squared[:], sums[b][:, 1:2], ACT.Square, bias=sums[b][:, 0:1])
            square(b, 1)
            stats = keep.tile([P, 3], F32, name="stats%d" % b)
            nc.gpsimd.tensor_scalar(
                stats[:, 0:1], squares[b][:, 0:1], total_squared[:], EPS * S * S / LAMBDA, ALU.subtract, ALU.add
            )
            nc.gpsimd.tensor_tensor(stats[:, 1:2], stats[:, 0:1], squares[b][:, 1:2], ALU.add)
            rstd[b] = stats[:, 2:3]
            nc.gpsimd.tensor_tensor(rstd[b], stats[:, 1:2], minus_half[:], ALU.pow)

        def mean_shift(b):
            shift[b] = keep.tile([P, 1], F32, name="shift%d" % b)
            nc.vector.tensor_scalar(shift[b][:], sums[b][:, 0:1], sums[b][:, 1:2], -LAMBDA / S, ALU.add, ALU.mult)

        def finish(b, h):
            weighted = log_truth[mirrored(b, h)]
            nc.vector.scalar_tensor_tensor(
                weighted[:],
                ld[b, h][:],
                shift[b][:],
                valid_bank[h][:],
                ALU.add,
                ALU.mult,
            )
            if b == BLOCKS - 1:
                nc.vector.tensor_scalar(result[b, h][:], weighted[:], rstd[b], None, ALU.mult)
            else:
                nc.scalar.activation(result[b, h][:], weighted[:], ACT.Copy, scale=rstd[b])
            nc.sync.dma_start(out[P * b : P * (b + 1), HALF * h : HALF * (h + 1)], result[b, h][:])

        difference(0, 0)
        square(0, 0)
        difference(0, 1)
        statistics(0)
        difference(1, 0)
        square(1, 0)
        mean_shift(0)
        difference(1, 1)
        statistics(1)
        finish(0, 0)
        mean_shift(1)
        for b, h in chunks[1:]:
            finish(b, h)
